import numpy as np
import ml_dtypes


def mxq(x, axis, fmt="e4m3"):
    dtype, down = {"e4m3": (ml_dtypes.float8_e4m3fn, 7), "e5m2": (ml_dtypes.float8_e5m2, 14)}[fmt]
    v = np.moveaxis(np.asarray(x, np.float32).astype(ml_dtypes.bfloat16).astype(np.float64), axis, -1)
    blocks = v.reshape(v.shape[:-1] + (-1, 32))
    amax = np.abs(blocks).max(-1, keepdims=True)
    byte = np.maximum(np.where(amax > 0, np.frexp(amax)[1] - 1 + 127, 0) - down, 1)
    scale = np.exp2(byte - 127.0)
    codes = (blocks / scale).astype(np.float32).astype(dtype).astype(np.float64)
    return np.moveaxis((codes * scale).reshape(v.shape), -1, axis)


WIDE = False


def mx_kscale(k):
    if not WIDE:
        return np.ones(k)
    levels = np.array([10, -10, 5, -5, 0])
    if k % 512:
        return np.exp2(np.random.permutation(np.resize(levels, k // 32))).repeat(32)
    a = np.empty((k // 512, 16))
    for p in range(k // 512):
        a[p, :8] = np.random.permutation(np.resize(levels, 8))
        for g in range(8):
            far = levels[np.abs(levels - a[p, g]) >= 10]
            a[p, g + 8] = far[np.random.randint(len(far))]
    return np.exp2(a.ravel()).repeat(32)


def f64(x):
    return np.asarray(x).astype(np.float64)


def striped(idx):
    return np.tile(idx.reshape(-1, 16).T, (8, 1)).astype(np.uint16)


def unstriped(offs):
    return offs[:16].T.reshape(-1).astype(np.int64)


def striped8(idx):
    return np.concatenate([x.reshape(-1, 16).T for x in idx]).astype(np.uint16)


def runs(offs, k):
    lists = np.stack([offs[16 * r : 16 * r + 16].T.reshape(-1) for r in range(8)]).astype(np.int64)
    return lists[np.arange(k) % 512 // 64]


def pack_weight(w):
    k, n = w.shape
    w = f64(np.asarray(w, np.float32).astype(ml_dtypes.bfloat16)).reshape(k // 32, 32, n)
    amax = np.abs(w).max(1)
    byte = np.clip(np.where(amax > 0, np.frexp(amax)[1] - 1 + 127 - 7, 1), 1, 254)
    scaled = (w * np.exp2(127.0 - byte)[:, None, :]).reshape(k, n).astype(np.float32)
    words = np.ascontiguousarray(scaled.reshape(k // 512, 128, 4, n).transpose(0, 1, 3, 2)).astype(ml_dtypes.float8_e4m3fn).view(np.uint8)
    return words, np.ascontiguousarray(byte.astype(np.uint8).reshape(k // 512, 16, n))


def unpack_weight(words, scales):
    g, p, n, _ = words.shape
    vals = np.ascontiguousarray(words).view(ml_dtypes.float8_e4m3fn).astype(np.float64) * np.repeat(np.exp2(scales.astype(np.float64) - 127.0), 8, axis=1)[..., None]
    return vals.transpose(0, 1, 3, 2).reshape(g * 512, n)

def planes(y):
    n, m = y.shape
    v = y.astype(np.float32).astype(ml_dtypes.bfloat16).astype(np.float64).reshape(n // 32, 32, m)
    top = np.abs(v).max(1)
    byte = np.clip(np.where(top > 0, np.frexp(top)[1] - 1 + 127 - 7, 1), 1, 254)
    codes = (v * np.exp2(127.0 - byte)[:, None, :]).reshape(n, m).astype(np.float32).astype(ml_dtypes.float8_e4m3fn).view(np.uint8)
    words = codes.reshape(n // 512, 128, 4, m).transpose(0, 1, 3, 2)
    return np.ascontiguousarray(words), np.ascontiguousarray(byte.astype(np.uint8).reshape(n // 512, 16, m))


K, T, S, N, H = 512, 2048, 512, 512, 512


def setup_inputs():
    n = np.random.standard_normal
    s = mx_kscale(K)[:, None]
    u = mx_kscale(H)
    packed_xT = pack_weight(n((K, T)) * s)
    packed_w1 = pack_weight(n((K, H)) / np.sqrt(K) / s)
    packed_w2 = pack_weight(n((K, H)) / np.sqrt(K) / s)
    packed_w3 = pack_weight(n((H, N)) / np.sqrt(H) / u[:, None])
    return {
        "x_words": packed_xT[0],
        "x_scales": packed_xT[1],
        "w1_words": packed_w1[0],
        "w1_scales": packed_w1[1],
        "w2_words": packed_w2[0],
        "w2_scales": packed_w2[1],
        "gn": (np.random.uniform(0.5, 1.5, (H, 1)) * u[:, None]).astype(np.float32),
        "w3_words": packed_w3[0],
        "w3_scales": packed_w3[1],
        "offs": striped(np.random.permutation(T)[:S]),
        "two": striped(np.random.permutation(T)[:S]),
        "n1": striped8(np.stack([np.random.permutation(S) for _ in range(8)])),
        "n2": striped8(np.stack([np.random.permutation(S) for _ in range(8)])),
        "n3": striped8(np.stack([np.random.permutation(S) for _ in range(8)])),
        "n4": striped8(np.stack([np.random.permutation(S) for _ in range(8)])),
        "n5": striped8(np.stack([np.random.permutation(S) for _ in range(8)])),
    }


def reference(x_words, x_scales, w1_words, w1_scales, w2_words, w2_scales, gn, w3_words, w3_scales, offs, two, n1, n2, n3, n4, n5):
    x_two = unpack_weight(x_words, x_scales)[:, unstriped(two)]
    d = unpack_weight(w2_words, w2_scales).T @ x_two
    xq = unpack_weight(x_words, x_scales)[:, unstriped(offs)]
    y = unpack_weight(w1_words, w1_scales).T @ xq
    z = f64(gn) * (d * (y[np.arange(H)[:, None], runs(n1, H)] - y) + 0.5 * ((d[np.arange(H)[:, None], runs(n3, H)]) * (y[np.arange(H)[:, None], runs(n2, H)] - y)))
    h = unpack_weight(w3_words, w3_scales).T @ mxq(z, 0, "e4m3")
    out_0 = h * (h[np.arange(N)[:, None], runs(n4, N)] - (h[np.arange(N)[:, None], runs(n5, N)]))
    return (out_0,) + planes(out_0)

@@ -1,0 +1,190 @@
+from contextlib import ExitStack
+
+import concourse.mybir as mybir
+
+K, T, S, N, H = 512, 2048, 512, 512, 512
+FLOPS = 3 * 2 * 512 * 512 * 512
+
+F32 = mybir.dt.float32
+BF16 = mybir.dt.bfloat16
+I32 = mybir.dt.int32
+U32 = mybir.dt.uint32
+U16 = mybir.dt.uint16
+U8 = mybir.dt.uint8
+FP8X4 = mybir.dt.float8_e4m3fn_x4
+MULT = mybir.AluOpType.mult
+ADD = mybir.AluOpType.add
+SUB = mybir.AluOpType.subtract
+COPY = mybir.ActivationFunctionType.Copy
+
+P = 128
+PACK = 4
+PIECES_Z = ((0, 256), (256, 128), (384, 128))
+PIECES_OUT = ((0, 256), (256, 128), (384, 128))
+
+
+def tile_picked_twlflowbwind_none_po_kernel(
+    tc, x_words, x_scales, w1_words, w1_scales, w2_words, w2_scales, gn, w3_words, w3_scales,
+    offs, two, n1, n2, n3, n4, n5, out_0, out_1, out_2,
+):
+    nc = tc.nc
+    with ExitStack() as ctx:
+        keep = ctx.enter_context(tc.tile_pool(name="keep", bufs=1))
+        psum = ctx.enter_context(tc.psum_pool(name="psum", bufs=1))
+
+        def sb(name, shape, dtype):
+            return keep.tile(shape, dtype, name=name, align_bytes=64)
+
+        def load_list(name, src):
+            tile = sb(name, [P, S // 16], U16)
+            nc.sync.dma_start(tile[:], src)
+            return tile
+
+        def load_words(name, src, cols):
+            tile = sb(name, [P, cols], I32)
+            nc.sync.dma_start(tile[:], src[0].rearrange("p n t -> p (n t)").bitcast(I32))
+            return tile
+
+        def load_scale_rows(tile, first, src):
+            for q in range(4):
+                nc.sync.dma_start(
+                    tile[32 * q + first : 32 * q + first + 4, :].bitcast(I32),
+                    src[0, 4 * q : 4 * q + 4, :].bitcast(I32),
+                )
+
+        def deal(engine, name, raw, dtype, run):
+            dealt = sb(name, [P, PACK * P], dtype)
+            engine.tensor_copy(
+                out=dealt[:].rearrange("p (t c i) -> p c t i", t=PACK, i=run),
+                in_=raw[:].rearrange("p (c i t) -> p c t i", t=PACK, i=run),
+            )
+            return dealt
+
+        def entries(lst, c0, n):
+            return lst[:, c0 // 16 : (c0 + n) // 16]
+
+        xs = sb("xs", [P, T], U8)
+        ws12 = sb("ws12", [P, H], U8)
+        ws3 = sb("ws3", [P, N], U8)
+        nc.vector.memset(xs[:].bitcast(I32), 0)
+        nc.vector.memset(ws12[:].bitcast(I32), 0)
+        nc.vector.memset(ws3[:].bitcast(I32), 0)
+
+        offs_t = load_list("offs_t", offs)
+        load_scale_rows(xs, 0, x_scales)
+        two_t = load_list("two_t", two)
+        xw = load_words("xw", x_words, T)
+        w1r = load_words("w1r", w1_words, H)
+        load_scale_rows(ws12, 0, w1_scales)
+        load_scale_rows(ws12, 4, w2_scales)
+        w2r = load_words("w2r", w2_words, H)
+        gain = sb("gain", [P, PACK], F32)
+        nc.sync.dma_start(gain[:], gn.rearrange("(p t) o -> p (t o)", t=PACK))
+        n1_t = load_list("n1_t", n1)
+        n2_t = load_list("n2_t", n2)
+        n3_t = load_list("n3_t", n3)
+        w3r = load_words("w3r", w3_words, N)
+        load_scale_rows(ws3, 0, w3_scales)
+        n4_t = load_list("n4_t", n4)
+        n5_t = load_list("n5_t", n5)
+
+        half_gain = sb("half_gain", [P, PACK], F32)
+        nc.scalar.activation(half_gain[:], gain[:], COPY, scale=0.5)
+
+        xs_y = sb("xs_y", [P, S], U8)
+        xs_d = sb("xs_d", [P, S], U8)
+        xw_y = sb("xw_y", [P, S], U32)
+        xw_d = sb("xw_d", [P, S], U32)
+        nc.vector.tensor_copy(xs_y[:], xs[:].indirect(offs_t[:]))
+        nc.vector.tensor_copy(xs_d[:], xs[:].indirect(two_t[:]))
+        nc.vector.tensor_copy(xw_y[:], xw[:].bitcast(U32).indirect(offs_t[:]))
+        w1 = deal(nc.vector, "w1", w1r, I32, 4)
+        s12 = deal(nc.vector, "s12", ws12, U8, 16)
+        nc.vector.tensor_copy(xw_d[:], xw[:].bitcast(U32).indirect(two_t[:]))
+        w2 = deal(nc.vector, "w2", w2r, I32, 4)
+
+        def product(bank, w, s, first, t, codes, scales):
+            cols = slice(t * P, (t + 1) * P)
+            nc.tensor.matmul_mx(
+                out=bank, lhsT=w[:, cols].bitcast(FP8X4), lhsT_scale=s[first:, cols],
+                rhs=codes.bitcast(FP8X4), rhs_scale=scales, start=True, stop=True,
+            )
+
+        y_bank = [psum.tile([P, S], F32, name="a%d" % t) for t in range(PACK)]
+        d_bank = [psum.tile([P, S], F32, name="b%d" % t) for t in range(PACK)]
+        for t in range(PACK):
+            product(y_bank[t][:], w1, s12, 0, t, xw_y[:], xs_y[:])
+        for t in range(PACK):
+            product(d_bank[t][:], w2, s12, 4, t, xw_d[:], xs_d[:])
+
+        y_win = [sb("y_win%d" % t, [P, S], F32) for t in range(PACK)]
+        y_own = [sb("y_own%d" % t, [P, S], F32) for t in range(PACK)]
+        d_win = [sb("d_win%d" % t, [P, S], F32) for t in range(PACK)]
+        for t in range(PACK):
+            nc.scalar.copy(y_win[t][:], y_bank[t][:])
+            nc.scalar.copy(y_own[t][:], y_bank[t][:])
+            nc.scalar.activation(d_win[t][:], d_bank[t][:], COPY, scale=half_gain[:, t : t + 1])
+
+        w3 = deal(nc.gpsimd, "w3", w3r, I32, 4)
+        s3 = deal(nc.gpsimd, "s3", ws3, U8, 16)
+
+        h_bank = [psum.tile([P, S], F32, name="a%d" % t) for t in range(PACK)]
+        h_win = [sb("h_win%d" % t, [P, S], F32) for t in range(PACK)]
+
+        for c0, n in PIECES_Z:
+            cols = slice(c0, c0 + n)
+            a = sb("a_%d" % c0, [P, PACK, n], F32)
+            b = sb("b_%d" % c0, [P, PACK, n], F32)
+            near = sb("near_%d" % c0, [P, PACK, n], F32)
+            far = sb("far_%d" % c0, [P, PACK, n], F32)
+            for t in range(PACK):
+                nc.vector.tensor_tensor(a[:, t, :], y_win[t][:].indirect(entries(n1_t, c0, n)), y_own[t][:, cols], SUB)
+                nc.vector.tensor_tensor(b[:, t, :], y_win[t][:].indirect(entries(n2_t, c0, n)), y_own[t][:, cols], SUB)
+                nc.vector.scalar_tensor_tensor(near[:, t, :], a[:, t, :], 2.0, d_win[t][:, cols], MULT, MULT)
+                nc.vector.tensor_tensor(far[:, t, :], d_win[t][:].indirect(entries(n3_t, c0, n)), b[:, t, :], MULT)
+            z = sb("z_%d" % c0, [P, n * PACK], BF16)
+            nc.vector.tensor_tensor(
+                z[:].rearrange("p (c i t) -> p c t i", t=PACK, i=2),
+                near[:].rearrange("p t (c i) -> p c t i", i=2),
+                far[:].rearrange("p t (c i) -> p c t i", i=2),
+                ADD,
+            )
+            z_codes = sb("z_codes%d" % c0, [P, n], U32)
+            z_scales = sb("z_scales%d" % c0, [P, n], U8)
+            nc.vector.quantize_mx(out=z_codes[:].bitcast(FP8X4), scales=z_scales[:], in_=z[:])
+            for t in range(PACK):
+                product(h_bank[t][:, cols], w3, s3, 0, t, z_codes[:], z_scales[:])
+            for t in range(PACK):
+                nc.scalar.copy(h_win[t][:, cols], h_bank[t][:, cols])
+
+        o_codes = sb("o_codes", [P, S], U32)
+        o_scales = sb("o_scales", [P, S], U8)
+        out_rows = out_0.rearrange("(p t) s -> p t s", t=PACK)
+        out_words = out_1[0].rearrange("p n t -> p (n t)").bitcast(I32)
+        for c0, n in PIECES_OUT:
+            cols = slice(c0, c0 + n)
+            h5 = sb("h5_%d" % c0, [P, PACK, n], F32)
+            diff = sb("diff_%d" % c0, [P, PACK, n], F32)
+            res = sb("res_%d" % c0, [P, PACK, n], F32)
+            for t in range(PACK):
+                nc.vector.tensor_copy(h5[:, t, :], h_win[t][:].indirect(entries(n5_t, c0, n)))
+            for t in range(PACK):
+                nc.vector.tensor_tensor(diff[:, t, :], h_win[t][:].indirect(entries(n4_t, c0, n)), h5[:, t, :], SUB)
+            for t in range(PACK):
+                nc.vector.tensor_tensor(res[:, t, :], diff[:, t, :], h_win[t][:, cols], MULT)
+            nc.sync.dma_start(out_rows[:, :, cols], res[:])
+            rounded = sb("rounded_%d" % c0, [P, n * PACK], BF16)
+            dst = rounded[:].rearrange("p (c i t) -> p c t i", t=PACK, i=2)
+            src = res[:].rearrange("p t (c i) -> p c t i", i=2)
+            if c0 + n < S:
+                nc.scalar.copy(dst, src)
+            else:
+                nc.vector.tensor_copy(dst, src)
+            nc.vector.quantize_mx(out=o_codes[:, cols].bitcast(FP8X4), scales=o_scales[:, cols], in_=rounded[:])
+            nc.sync.dma_start(out_words[:, cols], o_codes[:, cols].bitcast(I32))
+        for q in range(4):
+            queue = nc.scalar if q % 2 else nc.sync
+            queue.dma_start(
+                out_2[0, 4 * q : 4 * q + 4, :].bitcast(I32),
+                o_scales[32 * q : 32 * q + 4, :].bitcast(I32),
+            )

@@ -1,6 +1,7 @@
 from contextlib import ExitStack
 
 import concourse.mybir as mybir
+from concourse.masks import make_identity
 
 K, T, S, N, H = 512, 2048, 512, 512, 512
 FLOPS = 3 * 2 * 512 * 512 * 512
@@ -19,8 +20,10 @@ COPY = mybir.ActivationFunctionType.Copy
 
 P = 128
 PACK = 4
-PIECES_Z = ((0, 256), (256, 128), (384, 128))
-PIECES_OUT = ((0, 256), (256, 128), (384, 128))
+BLOCK = 128
+HALF = 256
+WIDE = 384
+SPARE = 256
 
 
 def tile_picked_twlflowbwind_none_po_kernel(
@@ -32,8 +35,8 @@ def tile_picked_twlflowbwind_none_po_kernel(
         keep = ctx.enter_context(tc.tile_pool(name="keep", bufs=1))
         psum = ctx.enter_context(tc.psum_pool(name="psum", bufs=1))
 
-        def sb(name, shape, dtype):
-            return keep.tile(shape, dtype, name=name, align_bytes=64)
+        def sb(name, shape, dtype, tag=None):
+            return keep.tile(shape, dtype, name=name, tag=tag or name, align_bytes=64)
 
         def load_list(name, src):
             tile = sb(name, [P, S // 16], U16)
@@ -45,9 +48,9 @@ def tile_picked_twlflowbwind_none_po_kernel(
             nc.sync.dma_start(tile[:], src[0].rearrange("p n t -> p (n t)").bitcast(I32))
             return tile
 
-        def load_scale_rows(tile, first, src):
+        def load_scale_rows(queue, tile, first, src):
             for q in range(4):
-                nc.sync.dma_start(
+                queue.dma_start(
                     tile[32 * q + first : 32 * q + first + 4, :].bitcast(I32),
                     src[0, 4 * q : 4 * q + 4, :].bitcast(I32),
                 )
@@ -64,27 +67,34 @@ def tile_picked_twlflowbwind_none_po_kernel(
             return lst[:, c0 // 16 : (c0 + n) // 16]
 
         xs = sb("xs", [P, T], U8)
-        ws12 = sb("ws12", [P, H], U8)
-        ws3 = sb("ws3", [P, N], U8)
+        ws1 = sb("ws1", [P, H], U8)
+        ws23 = sb("ws23", [P, H], U8)
         nc.vector.memset(xs[:].bitcast(I32), 0)
-        nc.vector.memset(ws12[:].bitcast(I32), 0)
-        nc.vector.memset(ws3[:].bitcast(I32), 0)
+        for plane in (ws1, ws23):
+            nc.gpsimd.memset(plane[:].bitcast(I32), 0)
+
+        y_win = [sb("y_win%d" % t, [P, S + SPARE], F32) for t in range(PACK)]
+        y_own = [sb("y_own%d" % t, [P, S], F32) for t in range(PACK)]
+        for t in range(PACK):
+            nc.vector.memset(y_win[t][:, S:], 0.0)
+        ident = sb("ident", [P, P], F32)
+        make_identity(nc, ident[:])
 
         offs_t = load_list("offs_t", offs)
-        load_scale_rows(xs, 0, x_scales)
         two_t = load_list("two_t", two)
-        xw = load_words("xw", x_words, T)
         w1r = load_words("w1r", w1_words, H)
-        load_scale_rows(ws12, 0, w1_scales)
-        load_scale_rows(ws12, 4, w2_scales)
+        load_scale_rows(nc.sync, xs, 0, x_scales)
+        xw = load_words("xw", x_words, T)
+        load_scale_rows(nc.sync, ws1, 0, w1_scales)
         w2r = load_words("w2r", w2_words, H)
-        gain = sb("gain", [P, PACK], F32)
-        nc.sync.dma_start(gain[:], gn.rearrange("(p t) o -> p (t o)", t=PACK))
+        w3r = load_words("w3r", w3_words, N)
         n1_t = load_list("n1_t", n1)
         n2_t = load_list("n2_t", n2)
+        load_scale_rows(nc.sync, ws23, 0, w2_scales)
+        load_scale_rows(nc.sync, ws23, 4, w3_scales)
+        gain = sb("gain", [P, PACK], F32)
+        nc.sync.dma_start(gain[:], gn.rearrange("(p t) o -> p (t o)", t=PACK))
         n3_t = load_list("n3_t", n3)
-        w3r = load_words("w3r", w3_words, N)
-        load_scale_rows(ws3, 0, w3_scales)
         n4_t = load_list("n4_t", n4)
         n5_t = load_list("n5_t", n5)
 
@@ -97,11 +107,14 @@ def tile_picked_twlflowbwind_none_po_kernel(
         xw_d = sb("xw_d", [P, S], U32)
         nc.vector.tensor_copy(xs_y[:], xs[:].indirect(offs_t[:]))
         nc.vector.tensor_copy(xs_d[:], xs[:].indirect(two_t[:]))
-        nc.vector.tensor_copy(xw_y[:], xw[:].bitcast(U32).indirect(offs_t[:]))
         w1 = deal(nc.vector, "w1", w1r, I32, 4)
-        s12 = deal(nc.vector, "s12", ws12, U8, 16)
+        for c0 in (0, HALF):
+            nc.vector.tensor_copy(xw_y[:, c0 : c0 + HALF], xw[:].bitcast(U32).indirect(entries(offs_t, c0, HALF)))
+        s1 = deal(nc.vector, "s1", ws1, U8, 16)
         nc.vector.tensor_copy(xw_d[:], xw[:].bitcast(U32).indirect(two_t[:]))
         w2 = deal(nc.vector, "w2", w2r, I32, 4)
+        w3 = deal(nc.gpsimd, "w3", w3r, I32, 4)
+        s23 = deal(nc.vector, "s23", ws23, U8, 16)
 
         def product(bank, w, s, first, t, codes, scales):
             cols = slice(t * P, (t + 1) * P)
@@ -111,77 +124,170 @@ def tile_picked_twlflowbwind_none_po_kernel(
             )
 
         y_bank = [psum.tile([P, S], F32, name="a%d" % t) for t in range(PACK)]
+        y_late = psum.tile([P, HALF], F32, name="b3")
+        product(y_bank[0][:, :HALF], w1, s1, 0, 0, xw_y[:, :HALF], xs_y[:, :HALF])
+        product(y_late[:], w1, s1, 0, 0, xw_y[:, HALF:], xs_y[:, HALF:])
+        for t in range(1, PACK):
+            product(y_bank[t][:], w1, s1, 0, t, xw_y[:], xs_y[:])
+        for c0, bank in ((0, y_bank[0][:, :HALF]), (HALF, y_late[:])):
+            nc.scalar.copy(y_win[0][:, c0 : c0 + HALF], bank)
+            nc.scalar.copy(y_own[0][:, c0 : c0 + HALF], bank)
+        for t in range(1, PACK):
+            nc.scalar.copy(y_win[t][:, :S], y_bank[t][:])
+            nc.scalar.copy(y_own[t][:], y_bank[t][:])
+
         d_bank = [psum.tile([P, S], F32, name="b%d" % t) for t in range(PACK)]
         for t in range(PACK):
-            product(y_bank[t][:], w1, s12, 0, t, xw_y[:], xs_y[:])
-        for t in range(PACK):
-            product(d_bank[t][:], w2, s12, 4, t, xw_d[:], xs_d[:])
-
-        y_win = [sb("y_win%d" % t, [P, S], F32) for t in range(PACK)]
-        y_own = [sb("y_own%d" % t, [P, S], F32) for t in range(PACK)]
+            product(d_bank[t][:], w2, s23, 0, t, xw_d[:], xs_d[:])
         d_win = [sb("d_win%d" % t, [P, S], F32) for t in range(PACK)]
-        for t in range(PACK):
-            nc.scalar.copy(y_win[t][:], y_bank[t][:])
-            nc.scalar.copy(y_own[t][:], y_bank[t][:])
-            nc.scalar.activation(d_win[t][:], d_bank[t][:], COPY, scale=half_gain[:, t : t + 1])
+        d_tail = sb("d_tail", [P, PACK, BLOCK], F32)
 
-        w3 = deal(nc.gpsimd, "w3", w3r, I32, 4)
-        s3 = deal(nc.gpsimd, "s3", ws3, U8, 16)
-
-        h_bank = [psum.tile([P, S], F32, name="a%d" % t) for t in range(PACK)]
-        h_win = [sb("h_win%d" % t, [P, S], F32) for t in range(PACK)]
-
-        for c0, n in PIECES_Z:
-            cols = slice(c0, c0 + n)
-            a = sb("a_%d" % c0, [P, PACK, n], F32)
-            b = sb("b_%d" % c0, [P, PACK, n], F32)
-            near = sb("near_%d" % c0, [P, PACK, n], F32)
-            far = sb("far_%d" % c0, [P, PACK, n], F32)
-            for t in range(PACK):
-                nc.vector.tensor_tensor(a[:, t, :], y_win[t][:].indirect(entries(n1_t, c0, n)), y_own[t][:, cols], SUB)
-                nc.vector.tensor_tensor(b[:, t, :], y_win[t][:].indirect(entries(n2_t, c0, n)), y_own[t][:, cols], SUB)
-                nc.vector.scalar_tensor_tensor(near[:, t, :], a[:, t, :], 2.0, d_win[t][:, cols], MULT, MULT)
-                nc.vector.tensor_tensor(far[:, t, :], d_win[t][:].indirect(entries(n3_t, c0, n)), b[:, t, :], MULT)
-            z = sb("z_%d" % c0, [P, n * PACK], BF16)
+        def step(out, lst, c0, n, t, window, plain):
             nc.vector.tensor_tensor(
-                z[:].rearrange("p (c i t) -> p c t i", t=PACK, i=2),
-                near[:].rearrange("p t (c i) -> p c t i", i=2),
-                far[:].rearrange("p t (c i) -> p c t i", i=2),
-                ADD,
+                out[:, t, :], window[t][:].indirect(entries(lst, c0, n)), plain[t][:, c0 : c0 + n], SUB
             )
-            z_codes = sb("z_codes%d" % c0, [P, n], U32)
-            z_scales = sb("z_scales%d" % c0, [P, n], U8)
-            nc.vector.quantize_mx(out=z_codes[:].bitcast(FP8X4), scales=z_scales[:], in_=z[:])
+
+        def steps_tile(c0, n):
+            both = sb("steps_%d" % c0, [P, 2, PACK, n], F32, "steps")
+            return both[:, 0], both[:, 1]
+
+        h_bank = [psum.tile([P, S], F32, name="b%d" % t) for t in range(PACK)]
+        h_win = [sb("h_win%d" % t, [P, S], F32) for t in range(PACK)]
+        h_own = sb("h_own", [P, PACK, S], F32)
+
+        def far_term(far, c0, n, b):
             for t in range(PACK):
-                product(h_bank[t][:, cols], w3, s3, 0, t, z_codes[:], z_scales[:])
+                nc.vector.tensor_tensor(far[t], d_win[t][:].indirect(entries(n3_t, c0, n)), b[:, t, :], MULT)
+
+        def turn(banks, term, first, last):
             for t in range(PACK):
-                nc.scalar.copy(h_win[t][:, cols], h_bank[t][:, cols])
+                for k, bank in enumerate(banks):
+                    nc.tensor.matmul(
+                        bank[:, t * P : (t + 1) * P], term[t][:, k * BLOCK : (k + 1) * BLOCK], ident[:],
+                        is_transpose=True, start=(first and t == 0), stop=(last and t == PACK - 1),
+                    )
+
+        def round_turned(name, bank):
+            turned = sb(name, [P, PACK * P], BF16)
+            nc.scalar.copy(
+                turned[:].rearrange("c (u p e) -> c u p e", u=2, e=2),
+                bank[:].rearrange("c (u e p) -> c u p e", u=2, e=2),
+            )
+            return turned
+
+        def turn_back(z, turned_blocks, bank_name):
+            count = len(turned_blocks)
+            back = psum.tile([P, count, 2, BLOCK], F32, name=bank_name)
+            for k, turned in enumerate(turned_blocks):
+                for u in range(2):
+                    nc.tensor.transpose(back[:, k, u, :], turned[:].bitcast(F32)[:, u * P : (u + 1) * P], ident[:])
+            nc.scalar.copy(z.rearrange("p (k c u) -> p k c u", k=count, u=2), back[:].rearrange("p k u c -> p k c u"))
+
+        def quantise_z(name, z, n):
+            codes = sb(name + "_codes", [P, n], U32)
+            scales = sb(name + "_scales", [P, n], U8)
+            nc.vector.quantize_mx(out=codes[:].bitcast(FP8X4), scales=scales[:], in_=z)
+            return codes, scales
+
+        a, b = steps_tile(0, WIDE)
+        near = [sb("near_wide%d" % t, [P, WIDE], F32) for t in range(PACK)]
+        for t in range(PACK):
+            step(a, n1_t, 0, WIDE, t, y_win, y_own)
+            nc.vector.scalar_tensor_tensor(
+                near[t][:], d_bank[t][:, :WIDE], gain[:, t : t + 1], a[:, t, :], MULT, MULT
+            )
+            step(b, n2_t, 0, WIDE, t, y_win, y_own)
+        for t in range(PACK):
+            nc.scalar.activation(d_win[t][:], d_bank[t][:], COPY, scale=half_gain[:, t : t + 1])
+            nc.scalar.activation(d_tail[:, t, :], d_bank[t][:, WIDE:], COPY, scale=gain[:, t : t + 1])
+        sum_bank = [psum.tile([P, S], F32, name="a%d" % k) for k in range(3)]
+        turn(sum_bank, near, True, False)
+        far = [sb("far_wide%d" % t, [P, WIDE], F32)[:] for t in range(PACK)]
+        far_term(far, 0, WIDE, b)
+        turn(sum_bank, far, False, True)
+        turned = [round_turned("turned_%d" % k, sum_bank[k]) for k in range(3)]
+        shared = sb("shared", [P, 6 * BLOCK], F32)
+        z_first = shared[:, 2 * BLOCK :]
+        z_second = sb("z_second", [P, 4 * BLOCK], F32)
+        turn_back(z_first, turned[:2], "a3")
+        turn_back(z_second[:, : 2 * BLOCK], turned[2:], "a0")
+
+        a, b = steps_tile(WIDE, BLOCK)
+        for out, lst in ((a, n1_t), (b, n2_t)):
+            for t in range(PACK):
+                step(out, lst, WIDE, BLOCK, t, y_own, y_win)
+        near = sb("near_tail", [P, PACK, BLOCK], F32)
+        nc.vector.tensor_tensor(near[:], a, d_tail[:], MULT)
+
+        codes, scales = quantise_z("z_first", z_first.bitcast(BF16), HALF)
+        for t in range(PACK):
+            product(h_bank[t][:, :HALF], w3, s23, 4, t, codes[:], scales[:])
+        for t in range(PACK):
+            nc.scalar.copy(h_win[t][:, :HALF], h_bank[t][:, :HALF])
+
+        far = shared[:, : 4 * BLOCK].rearrange("p (t c) -> p t c", t=PACK)
+        far_term([far[:, t, :] for t in range(PACK)], WIDE, BLOCK, b)
+        nc.vector.tensor_tensor(
+            z_second[:, 2 * BLOCK :].bitcast(BF16).rearrange("p (c i t) -> p c t i", t=PACK, i=2),
+            near[:].rearrange("p t (c i) -> p c t i", i=2),
+            far.rearrange("p t (c i) -> p c t i", i=2),
+            ADD,
+        )
+        codes, scales = quantise_z("z_second", z_second[:].bitcast(BF16), HALF)
+        for t in range(PACK):
+            product(h_bank[t][:, HALF:], w3, s23, 4, t, codes[:], scales[:])
+        for t in range(PACK):
+            nc.scalar.copy(h_win[t][:, HALF:], h_bank[t][:, HALF:])
+        for t in range(PACK):
+            nc.scalar.copy(h_own[:, t, :], h_bank[t][:])
 
         o_codes = sb("o_codes", [P, S], U32)
         o_scales = sb("o_scales", [P, S], U8)
         out_rows = out_0.rearrange("(p t) s -> p t s", t=PACK)
         out_words = out_1[0].rearrange("p n t -> p (n t)").bitcast(I32)
-        for c0, n in PIECES_OUT:
-            cols = slice(c0, c0 + n)
-            h5 = sb("h5_%d" % c0, [P, PACK, n], F32)
-            diff = sb("diff_%d" % c0, [P, PACK, n], F32)
-            res = sb("res_%d" % c0, [P, PACK, n], F32)
+
+        def fetch_h5(c0):
+            h5 = sb("h5_%d" % c0, [P, PACK, HALF], F32, "h5")
             for t in range(PACK):
-                nc.vector.tensor_copy(h5[:, t, :], h_win[t][:].indirect(entries(n5_t, c0, n)))
+                nc.vector.tensor_copy(h5[:, t, :], h_win[t][:].indirect(entries(n5_t, c0, HALF)))
+            return h5
+
+        def difference(c0, n, h5, diff):
             for t in range(PACK):
                 nc.vector.tensor_tensor(diff[:, t, :], h_win[t][:].indirect(entries(n4_t, c0, n)), h5[:, t, :], SUB)
-            for t in range(PACK):
-                nc.vector.tensor_tensor(res[:, t, :], diff[:, t, :], h_win[t][:, cols], MULT)
+            return diff
+
+        def finish(c0, n, diff, mult_engine, last):
+            cols = slice(c0, c0 + n)
+            res = sb("res_%d" % c0, [P, PACK, n], F32)
+            mult_engine.tensor_tensor(res[:], diff, h_own[:, :, cols], MULT)
             nc.sync.dma_start(out_rows[:, :, cols], res[:])
             rounded = sb("rounded_%d" % c0, [P, n * PACK], BF16)
             dst = rounded[:].rearrange("p (c i t) -> p c t i", t=PACK, i=2)
             src = res[:].rearrange("p t (c i) -> p c t i", i=2)
-            if c0 + n < S:
-                nc.scalar.copy(dst, src)
-            else:
+            if last:
                 nc.vector.tensor_copy(dst, src)
+            else:
+                nc.scalar.copy(dst, src)
+            return rounded
+
+        def hand_on(c0, n, rounded):
+            cols = slice(c0, c0 + n)
             nc.vector.quantize_mx(out=o_codes[:, cols].bitcast(FP8X4), scales=o_scales[:, cols], in_=rounded[:])
             nc.sync.dma_start(out_words[:, cols], o_codes[:, cols].bitcast(I32))
+
+        h5 = fetch_h5(0)
+        diff_a = difference(0, HALF, h5[:], sb("diff_a", [P, PACK, HALF], F32, "diff")[:])
+        h5 = fetch_h5(HALF)
+        rounded_a = finish(0, HALF, diff_a, nc.gpsimd, False)
+        diff_bc = sb("diff_bc", [P, 2, PACK, BLOCK], F32, "diff")
+        diff_b = difference(HALF, BLOCK, h5[:, :, :BLOCK], diff_bc[:, 0])
+        rounded_b = finish(HALF, BLOCK, diff_b, nc.vector, False)
+        diff_c = difference(WIDE, BLOCK, h5[:, :, BLOCK:], diff_bc[:, 1])
+        hand_on(0, HALF, rounded_a)
+        rounded_c = finish(3 * BLOCK, BLOCK, diff_c, nc.vector, True)
+        hand_on(HALF, BLOCK, rounded_b)
+        hand_on(3 * BLOCK, BLOCK, rounded_c)
         for q in range(4):
             queue = nc.scalar if q % 2 else nc.sync
             queue.dma_start(

@@ -48,9 +48,9 @@ def tile_picked_twlflowbwind_none_po_kernel(
             nc.sync.dma_start(tile[:], src[0].rearrange("p n t -> p (n t)").bitcast(I32))
             return tile
 
-        def load_scale_rows(queue, tile, first, src):
+        def load_scale_rows(queues, tile, first, src):
             for q in range(4):
-                queue.dma_start(
+                queues[q % len(queues)].dma_start(
                     tile[32 * q + first : 32 * q + first + 4, :].bitcast(I32),
                     src[0, 4 * q : 4 * q + 4, :].bitcast(I32),
                 )
@@ -68,33 +68,35 @@ def tile_picked_twlflowbwind_none_po_kernel(
 
         xs = sb("xs", [P, T], U8)
         ws1 = sb("ws1", [P, H], U8)
-        ws23 = sb("ws23", [P, H], U8)
+        ws2 = sb("ws2", [P, H], U8)
+        ws3 = sb("ws3", [P, N], U8)
         nc.vector.memset(xs[:].bitcast(I32), 0)
-        for plane in (ws1, ws23):
+        for plane in (ws2, ws1):
             nc.gpsimd.memset(plane[:].bitcast(I32), 0)
+        nc.vector.memset(ws3[:].bitcast(I32), 0)
+        ident = sb("ident", [P, P], F32)
+        make_identity(nc, ident[:])
 
         y_win = [sb("y_win%d" % t, [P, S + SPARE], F32) for t in range(PACK)]
         y_own = [sb("y_own%d" % t, [P, S], F32) for t in range(PACK)]
         for t in range(PACK):
             nc.vector.memset(y_win[t][:, S:], 0.0)
-        ident = sb("ident", [P, P], F32)
-        make_identity(nc, ident[:])
 
         offs_t = load_list("offs_t", offs)
         two_t = load_list("two_t", two)
         w1r = load_words("w1r", w1_words, H)
-        load_scale_rows(nc.sync, xs, 0, x_scales)
+        load_scale_rows((nc.sync, nc.scalar), xs, 0, x_scales)
         xw = load_words("xw", x_words, T)
-        load_scale_rows(nc.sync, ws1, 0, w1_scales)
+        load_scale_rows((nc.sync,), ws1, 0, w1_scales)
         w2r = load_words("w2r", w2_words, H)
         w3r = load_words("w3r", w3_words, N)
         n1_t = load_list("n1_t", n1)
         n2_t = load_list("n2_t", n2)
-        load_scale_rows(nc.sync, ws23, 0, w2_scales)
-        load_scale_rows(nc.sync, ws23, 4, w3_scales)
+        load_scale_rows((nc.gpsimd, nc.gpsimd, nc.gpsimd, nc.sync), ws2, 0, w2_scales)
         gain = sb("gain", [P, PACK], F32)
         nc.sync.dma_start(gain[:], gn.rearrange("(p t) o -> p (t o)", t=PACK))
         n3_t = load_list("n3_t", n3)
+        load_scale_rows((nc.sync,), ws3, 0, w3_scales)
         n4_t = load_list("n4_t", n4)
         n5_t = load_list("n5_t", n5)
 
@@ -110,11 +112,12 @@ def tile_picked_twlflowbwind_none_po_kernel(
         w1 = deal(nc.vector, "w1", w1r, I32, 4)
         for c0 in (0, HALF):
             nc.vector.tensor_copy(xw_y[:, c0 : c0 + HALF], xw[:].bitcast(U32).indirect(entries(offs_t, c0, HALF)))
-        s1 = deal(nc.vector, "s1", ws1, U8, 16)
+        s1 = deal(nc.gpsimd, "s1", ws1, U8, 16)
         nc.vector.tensor_copy(xw_d[:], xw[:].bitcast(U32).indirect(two_t[:]))
         w2 = deal(nc.vector, "w2", w2r, I32, 4)
         w3 = deal(nc.gpsimd, "w3", w3r, I32, 4)
-        s23 = deal(nc.vector, "s23", ws23, U8, 16)
+        s2 = deal(nc.gpsimd, "s2", ws2, U8, 16)
+        s3 = deal(nc.vector, "s3", ws3, U8, 16)
 
         def product(bank, w, s, first, t, codes, scales):
             cols = slice(t * P, (t + 1) * P)
@@ -138,18 +141,14 @@ def tile_picked_twlflowbwind_none_po_kernel(
 
         d_bank = [psum.tile([P, S], F32, name="b%d" % t) for t in range(PACK)]
         for t in range(PACK):
-            product(d_bank[t][:], w2, s23, 0, t, xw_d[:], xs_d[:])
+            product(d_bank[t][:], w2, s2, 0, t, xw_d[:], xs_d[:])
         d_win = [sb("d_win%d" % t, [P, S], F32) for t in range(PACK)]
         d_tail = sb("d_tail", [P, PACK, BLOCK], F32)
 
         def step(out, lst, c0, n, t, window, plain):
             nc.vector.tensor_tensor(
-                out[:, t, :], window[t][:].indirect(entries(lst, c0, n)), plain[t][:, c0 : c0 + n], SUB
+                out, window[t][:].indirect(entries(lst, c0, n)), plain[t][:, c0 : c0 + n], SUB
             )
-
-        def steps_tile(c0, n):
-            both = sb("steps_%d" % c0, [P, 2, PACK, n], F32, "steps")
-            return both[:, 0], both[:, 1]
 
         h_bank = [psum.tile([P, S], F32, name="b%d" % t) for t in range(PACK)]
         h_win = [sb("h_win%d" % t, [P, S], F32) for t in range(PACK)]
@@ -157,7 +156,7 @@ def tile_picked_twlflowbwind_none_po_kernel(
 
         def far_term(far, c0, n, b):
             for t in range(PACK):
-                nc.vector.tensor_tensor(far[t], d_win[t][:].indirect(entries(n3_t, c0, n)), b[:, t, :], MULT)
+                nc.vector.tensor_tensor(far[t], d_win[t][:].indirect(entries(n3_t, c0, n)), b[t], MULT)
 
         def turn(banks, term, first, last):
             for t in range(PACK):
@@ -189,14 +188,14 @@ def tile_picked_twlflowbwind_none_po_kernel(
             nc.vector.quantize_mx(out=codes[:].bitcast(FP8X4), scales=scales[:], in_=z)
             return codes, scales
 
-        a, b = steps_tile(0, WIDE)
+        steps = sb("steps_wide", [P, 6, WIDE], F32, "steps")
+        a = [steps[:, t, :] for t in range(PACK)]
+        b = [steps[:, (PACK + t) % 6, :] for t in range(PACK)]
         near = [sb("near_wide%d" % t, [P, WIDE], F32) for t in range(PACK)]
         for t in range(PACK):
-            step(a, n1_t, 0, WIDE, t, y_win, y_own)
-            nc.vector.scalar_tensor_tensor(
-                near[t][:], d_bank[t][:, :WIDE], gain[:, t : t + 1], a[:, t, :], MULT, MULT
-            )
-            step(b, n2_t, 0, WIDE, t, y_win, y_own)
+            step(a[t], n1_t, 0, WIDE, t, y_win, y_own)
+            nc.vector.scalar_tensor_tensor(near[t][:], d_bank[t][:, :WIDE], gain[:, t : t + 1], a[t], MULT, MULT)
+            step(b[t], n2_t, 0, WIDE, t, y_win, y_own)
         for t in range(PACK):
             nc.scalar.activation(d_win[t][:], d_bank[t][:], COPY, scale=half_gain[:, t : t + 1])
             nc.scalar.activation(d_tail[:, t, :], d_bank[t][:, WIDE:], COPY, scale=gain[:, t : t + 1])
@@ -212,16 +211,18 @@ def tile_picked_twlflowbwind_none_po_kernel(
         turn_back(z_first, turned[:2], "a3")
         turn_back(z_second[:, : 2 * BLOCK], turned[2:], "a0")
 
-        a, b = steps_tile(WIDE, BLOCK)
-        for out, lst in ((a, n1_t), (b, n2_t)):
+        steps = sb("steps_tail", [P, 2, PACK, BLOCK], F32, "steps")
+        for which, lst in enumerate((n1_t, n2_t)):
             for t in range(PACK):
-                step(out, lst, WIDE, BLOCK, t, y_own, y_win)
+                step(steps[:, which, t, :], lst, WIDE, BLOCK, t, y_own, y_win)
+        a = steps[:, 0]
+        b = [steps[:, 1, t, :] for t in range(PACK)]
         near = sb("near_tail", [P, PACK, BLOCK], F32)
         nc.vector.tensor_tensor(near[:], a, d_tail[:], MULT)
 
         codes, scales = quantise_z("z_first", z_first.bitcast(BF16), HALF)
         for t in range(PACK):
-            product(h_bank[t][:, :HALF], w3, s23, 4, t, codes[:], scales[:])
+            product(h_bank[t][:, :HALF], w3, s3, 0, t, codes[:], scales[:])
         for t in range(PACK):
             nc.scalar.copy(h_win[t][:, :HALF], h_bank[t][:, :HALF])
 
@@ -235,7 +236,7 @@ def tile_picked_twlflowbwind_none_po_kernel(
         )
         codes, scales = quantise_z("z_second", z_second[:].bitcast(BF16), HALF)
         for t in range(PACK):
-            product(h_bank[t][:, HALF:], w3, s23, 4, t, codes[:], scales[:])
+            product(h_bank[t][:, HALF:], w3, s3, 0, t, codes[:], scales[:])
         for t in range(PACK):
             nc.scalar.copy(h_win[t][:, HALF:], h_bank[t][:, HALF:])
         for t in range(PACK):

from contextlib import ExitStack

import concourse.mybir as mybir
from concourse.masks import make_identity

K, T, S, N, H = 512, 2048, 512, 512, 512
FLOPS = 3 * 2 * 512 * 512 * 512

F32 = mybir.dt.float32
BF16 = mybir.dt.bfloat16
I32 = mybir.dt.int32
U32 = mybir.dt.uint32
U16 = mybir.dt.uint16
U8 = mybir.dt.uint8
FP8X4 = mybir.dt.float8_e4m3fn_x4
MULT = mybir.AluOpType.mult
ADD = mybir.AluOpType.add
SUB = mybir.AluOpType.subtract
COPY = mybir.ActivationFunctionType.Copy

P = 128
PACK = 4
BLOCK = 128
HALF = 256
WIDE = 384
SPARE = 256


def tile_picked_twlflowbwind_none_po_kernel(
    tc, x_words, x_scales, w1_words, w1_scales, w2_words, w2_scales, gn, w3_words, w3_scales,
    offs, two, n1, n2, n3, n4, n5, out_0, out_1, out_2,
):
    nc = tc.nc
    with ExitStack() as ctx:
        keep = ctx.enter_context(tc.tile_pool(name="keep", bufs=1))
        psum = ctx.enter_context(tc.psum_pool(name="psum", bufs=1))

        def sb(name, shape, dtype, tag=None):
            return keep.tile(shape, dtype, name=name, tag=tag or name, align_bytes=64)

        def load_list(name, src):
            tile = sb(name, [P, S // 16], U16)
            nc.sync.dma_start(tile[:], src)
            return tile

        def load_words(name, src, cols):
            tile = sb(name, [P, cols], I32)
            nc.sync.dma_start(tile[:], src[0].rearrange("p n t -> p (n t)").bitcast(I32))
            return tile

        def load_scale_rows(queues, tile, first, src):
            for q in range(4):
                queues[q % len(queues)].dma_start(
                    tile[32 * q + first : 32 * q + first + 4, :].bitcast(I32),
                    src[0, 4 * q : 4 * q + 4, :].bitcast(I32),
                )

        def deal(engine, name, raw, dtype, run):
            dealt = sb(name, [P, PACK * P], dtype)
            engine.tensor_copy(
                out=dealt[:].rearrange("p (t c i) -> p c t i", t=PACK, i=run),
                in_=raw[:].rearrange("p (c i t) -> p c t i", t=PACK, i=run),
            )
            return dealt

        def entries(lst, c0, n):
            return lst[:, c0 // 16 : (c0 + n) // 16]

        xs = sb("xs", [P, T], U8)
        ws1 = sb("ws1", [P, H], U8)
        ws2 = sb("ws2", [P, H], U8)
        ws3 = sb("ws3", [P, N], U8)
        nc.vector.memset(xs[:].bitcast(I32), 0)
        for plane in (ws2, ws1):
            nc.gpsimd.memset(plane[:].bitcast(I32), 0)
        nc.vector.memset(ws3[:].bitcast(I32), 0)
        ident = sb("ident", [P, P], F32)
        make_identity(nc, ident[:])

        y_win = [sb("y_win%d" % t, [P, S + SPARE], F32) for t in range(PACK)]
        y_own = [sb("y_own%d" % t, [P, S], F32) for t in range(PACK)]
        for t in range(PACK):
            nc.vector.memset(y_win[t][:, S:], 0.0)

        offs_t = load_list("offs_t", offs)
        two_t = load_list("two_t", two)
        w1r = load_words("w1r", w1_words, H)
        load_scale_rows((nc.sync, nc.scalar), xs, 0, x_scales)
        xw = load_words("xw", x_words, T)
        load_scale_rows((nc.sync,), ws1, 0, w1_scales)
        w2r = load_words("w2r", w2_words, H)
        w3r = load_words("w3r", w3_words, N)
        n1_t = load_list("n1_t", n1)
        n2_t = load_list("n2_t", n2)
        load_scale_rows((nc.gpsimd, nc.gpsimd, nc.gpsimd, nc.sync), ws2, 0, w2_scales)
        gain = sb("gain", [P, PACK], F32)
        nc.sync.dma_start(gain[:], gn.rearrange("(p t) o -> p (t o)", t=PACK))
        n3_t = load_list("n3_t", n3)
        load_scale_rows((nc.sync,), ws3, 0, w3_scales)
        n4_t = load_list("n4_t", n4)
        n5_t = load_list("n5_t", n5)

        half_gain = sb("half_gain", [P, PACK], F32)
        nc.scalar.activation(half_gain[:], gain[:], COPY, scale=0.5)

        xs_y = sb("xs_y", [P, S], U8)
        xs_d = sb("xs_d", [P, S], U8)
        xw_y = sb("xw_y", [P, S], U32)
        xw_d = sb("xw_d", [P, S], U32)
        nc.vector.tensor_copy(xs_y[:], xs[:].indirect(offs_t[:]))
        nc.vector.tensor_copy(xs_d[:], xs[:].indirect(two_t[:]))
        w1 = deal(nc.vector, "w1", w1r, I32, 4)
        for c0 in (0, HALF):
            nc.vector.tensor_copy(xw_y[:, c0 : c0 + HALF], xw[:].bitcast(U32).indirect(entries(offs_t, c0, HALF)))
        s1 = deal(nc.gpsimd, "s1", ws1, U8, 16)
        nc.vector.tensor_copy(xw_d[:], xw[:].bitcast(U32).indirect(two_t[:]))
        w2 = deal(nc.vector, "w2", w2r, I32, 4)
        w3 = deal(nc.gpsimd, "w3", w3r, I32, 4)
        s2 = deal(nc.gpsimd, "s2", ws2, U8, 16)
        s3 = deal(nc.vector, "s3", ws3, U8, 16)

        def product(bank, w, s, first, t, codes, scales):
            cols = slice(t * P, (t + 1) * P)
            nc.tensor.matmul_mx(
                out=bank, lhsT=w[:, cols].bitcast(FP8X4), lhsT_scale=s[first:, cols],
                rhs=codes.bitcast(FP8X4), rhs_scale=scales, start=True, stop=True,
            )

        y_bank = [psum.tile([P, S], F32, name="a%d" % t) for t in range(PACK)]
        y_late = psum.tile([P, HALF], F32, name="b3")
        product(y_bank[0][:, :HALF], w1, s1, 0, 0, xw_y[:, :HALF], xs_y[:, :HALF])
        product(y_late[:], w1, s1, 0, 0, xw_y[:, HALF:], xs_y[:, HALF:])
        for t in range(1, PACK):
            product(y_bank[t][:], w1, s1, 0, t, xw_y[:], xs_y[:])
        for c0, bank in ((0, y_bank[0][:, :HALF]), (HALF, y_late[:])):
            nc.scalar.copy(y_win[0][:, c0 : c0 + HALF], bank)
            nc.scalar.copy(y_own[0][:, c0 : c0 + HALF], bank)
        for t in range(1, PACK):
            nc.scalar.copy(y_win[t][:, :S], y_bank[t][:])
            nc.scalar.copy(y_own[t][:], y_bank[t][:])

        d_bank = [psum.tile([P, S], F32, name="b%d" % t) for t in range(PACK)]
        for t in range(PACK):
            product(d_bank[t][:], w2, s2, 0, t, xw_d[:], xs_d[:])
        d_win = [sb("d_win%d" % t, [P, S], F32) for t in range(PACK)]
        d_tail = sb("d_tail", [P, PACK, BLOCK], F32)

        def step(out, lst, c0, n, t, window, plain):
            nc.vector.tensor_tensor(
                out, window[t][:].indirect(entries(lst, c0, n)), plain[t][:, c0 : c0 + n], SUB
            )

        h_bank = [psum.tile([P, S], F32, name="b%d" % t) for t in range(PACK)]
        h_win = [sb("h_win%d" % t, [P, S], F32) for t in range(PACK)]
        h_own = sb("h_own", [P, PACK, S], F32)

        def far_term(far, c0, n, b):
            for t in range(PACK):
                nc.vector.tensor_tensor(far[t], d_win[t][:].indirect(entries(n3_t, c0, n)), b[t], MULT)

        def turn(banks, term, first, last):
            for t in range(PACK):
                for k, bank in enumerate(banks):
                    nc.tensor.matmul(
                        bank[:, t * P : (t + 1) * P], term[t][:, k * BLOCK : (k + 1) * BLOCK], ident[:],
                        is_transpose=True, start=(first and t == 0), stop=(last and t == PACK - 1),
                    )

        def round_turned(name, bank):
            turned = sb(name, [P, PACK * P], BF16)
            nc.scalar.copy(
                turned[:].rearrange("c (u p e) -> c u p e", u=2, e=2),
                bank[:].rearrange("c (u e p) -> c u p e", u=2, e=2),
            )
            return turned

        def turn_back(z, turned_blocks, bank_name):
            count = len(turned_blocks)
            back = psum.tile([P, count, 2, BLOCK], F32, name=bank_name)
            for k, turned in enumerate(turned_blocks):
                for u in range(2):
                    nc.tensor.transpose(back[:, k, u, :], turned[:].bitcast(F32)[:, u * P : (u + 1) * P], ident[:])
            nc.scalar.copy(z.rearrange("p (k c u) -> p k c u", k=count, u=2), back[:].rearrange("p k u c -> p k c u"))

        def quantise_z(name, z, n):
            codes = sb(name + "_codes", [P, n], U32)
            scales = sb(name + "_scales", [P, n], U8)
            nc.vector.quantize_mx(out=codes[:].bitcast(FP8X4), scales=scales[:], in_=z)
            return codes, scales

        steps = sb("steps_wide", [P, 6, WIDE], F32, "steps")
        a = [steps[:, t, :] for t in range(PACK)]
        b = [steps[:, (PACK + t) % 6, :] for t in range(PACK)]
        near = [sb("near_wide%d" % t, [P, WIDE], F32) for t in range(PACK)]
        for t in range(PACK):
            step(a[t], n1_t, 0, WIDE, t, y_win, y_own)
            nc.vector.scalar_tensor_tensor(near[t][:], d_bank[t][:, :WIDE], gain[:, t : t + 1], a[t], MULT, MULT)
            step(b[t], n2_t, 0, WIDE, t, y_win, y_own)
        for t in range(PACK):
            nc.scalar.activation(d_win[t][:], d_bank[t][:], COPY, scale=half_gain[:, t : t + 1])
            nc.scalar.activation(d_tail[:, t, :], d_bank[t][:, WIDE:], COPY, scale=gain[:, t : t + 1])
        sum_bank = [psum.tile([P, S], F32, name="a%d" % k) for k in range(3)]
        turn(sum_bank, near, True, False)
        far = [sb("far_wide%d" % t, [P, WIDE], F32)[:] for t in range(PACK)]
        far_term(far, 0, WIDE, b)
        turn(sum_bank, far, False, True)
        turned = [round_turned("turned_%d" % k, sum_bank[k]) for k in range(3)]
        shared = sb("shared", [P, 6 * BLOCK], F32)
        z_first = shared[:, 2 * BLOCK :]
        z_second = sb("z_second", [P, 4 * BLOCK], F32)
        turn_back(z_first, turned[:2], "a3")
        turn_back(z_second[:, : 2 * BLOCK], turned[2:], "a0")

        steps = sb("steps_tail", [P, 2, PACK, BLOCK], F32, "steps")
        for which, lst in enumerate((n1_t, n2_t)):
            for t in range(PACK):
                step(steps[:, which, t, :], lst, WIDE, BLOCK, t, y_own, y_win)
        a = steps[:, 0]
        b = [steps[:, 1, t, :] for t in range(PACK)]
        near = sb("near_tail", [P, PACK, BLOCK], F32)
        nc.vector.tensor_tensor(near[:], a, d_tail[:], MULT)

        codes, scales = quantise_z("z_first", z_first.bitcast(BF16), HALF)
        for t in range(PACK):
            product(h_bank[t][:, :HALF], w3, s3, 0, t, codes[:], scales[:])
        for t in range(PACK):
            nc.scalar.copy(h_win[t][:, :HALF], h_bank[t][:, :HALF])

        far = shared[:, : 4 * BLOCK].rearrange("p (t c) -> p t c", t=PACK)
        far_term([far[:, t, :] for t in range(PACK)], WIDE, BLOCK, b)
        nc.vector.tensor_tensor(
            z_second[:, 2 * BLOCK :].bitcast(BF16).rearrange("p (c i t) -> p c t i", t=PACK, i=2),
            near[:].rearrange("p t (c i) -> p c t i", i=2),
            far.rearrange("p t (c i) -> p c t i", i=2),
            ADD,
        )
        codes, scales = quantise_z("z_second", z_second[:].bitcast(BF16), HALF)
        for t in range(PACK):
            product(h_bank[t][:, HALF:], w3, s3, 0, t, codes[:], scales[:])
        for t in range(PACK):
            nc.scalar.copy(h_win[t][:, HALF:], h_bank[t][:, HALF:])
        for t in range(PACK):
            nc.scalar.copy(h_own[:, t, :], h_bank[t][:])

        o_codes = sb("o_codes", [P, S], U32)
        o_scales = sb("o_scales", [P, S], U8)
        out_rows = out_0.rearrange("(p t) s -> p t s", t=PACK)
        out_words = out_1[0].rearrange("p n t -> p (n t)").bitcast(I32)

        def fetch_h5(c0):
            h5 = sb("h5_%d" % c0, [P, PACK, HALF], F32, "h5")
            for t in range(PACK):
                nc.vector.tensor_copy(h5[:, t, :], h_win[t][:].indirect(entries(n5_t, c0, HALF)))
            return h5

        def difference(c0, n, h5, diff):
            for t in range(PACK):
                nc.vector.tensor_tensor(diff[:, t, :], h_win[t][:].indirect(entries(n4_t, c0, n)), h5[:, t, :], SUB)
            return diff

        def finish(c0, n, diff, mult_engine, last):
            cols = slice(c0, c0 + n)
            res = sb("res_%d" % c0, [P, PACK, n], F32)
            mult_engine.tensor_tensor(res[:], diff, h_own[:, :, cols], MULT)
            nc.sync.dma_start(out_rows[:, :, cols], res[:])
            rounded = sb("rounded_%d" % c0, [P, n * PACK], BF16)
            dst = rounded[:].rearrange("p (c i t) -> p c t i", t=PACK, i=2)
            src = res[:].rearrange("p t (c i) -> p c t i", i=2)
            if last:
                nc.vector.tensor_copy(dst, src)
            else:
                nc.scalar.copy(dst, src)
            return rounded

        def hand_on(c0, n, rounded):
            cols = slice(c0, c0 + n)
            nc.vector.quantize_mx(out=o_codes[:, cols].bitcast(FP8X4), scales=o_scales[:, cols], in_=rounded[:])
            nc.sync.dma_start(out_words[:, cols], o_codes[:, cols].bitcast(I32))

        h5 = fetch_h5(0)
        diff_a = difference(0, HALF, h5[:], sb("diff_a", [P, PACK, HALF], F32, "diff")[:])
        h5 = fetch_h5(HALF)
        rounded_a = finish(0, HALF, diff_a, nc.gpsimd, False)
        diff_bc = sb("diff_bc", [P, 2, PACK, BLOCK], F32, "diff")
        diff_b = difference(HALF, BLOCK, h5[:, :, :BLOCK], diff_bc[:, 0])
        rounded_b = finish(HALF, BLOCK, diff_b, nc.vector, False)
        diff_c = difference(WIDE, BLOCK, h5[:, :, BLOCK:], diff_bc[:, 1])
        hand_on(0, HALF, rounded_a)
        rounded_c = finish(3 * BLOCK, BLOCK, diff_c, nc.vector, True)
        hand_on(HALF, BLOCK, rounded_b)
        hand_on(3 * BLOCK, BLOCK, rounded_c)
        for q in range(4):
            queue = nc.scalar if q % 2 else nc.sync
            queue.dma_start(
                out_2[0, 4 * q : 4 * q + 4, :].bitcast(I32),
                o_scales[32 * q : 32 * q + 4, :].bitcast(I32),
            )
